import numpy as np
import ml_dtypes


def mxq(x, axis, fmt="e4m3"):
    dtype, down = {"e4m3": (ml_dtypes.float8_e4m3fn, 7), "e5m2": (ml_dtypes.float8_e5m2, 14)}[fmt]
    v = np.moveaxis(np.asarray(x, np.float32).astype(ml_dtypes.bfloat16).astype(np.float64), axis, -1)
    blocks = v.reshape(v.shape[:-1] + (-1, 32))
    amax = np.abs(blocks).max(-1, keepdims=True)
    byte = np.maximum(np.where(amax > 0, np.frexp(amax)[1] - 1 + 127, 0) - down, 1)
    scale = np.exp2(byte - 127.0)
    codes = (blocks / scale).astype(np.float32).astype(dtype).astype(np.float64)
    return np.moveaxis((codes * scale).reshape(v.shape), -1, axis)


WIDE = False


def mx_kscale(k):
    if not WIDE:
        return np.ones(k)
    levels = np.array([10, -10, 5, -5, 0])
    if k % 512:
        return np.exp2(np.random.permutation(np.resize(levels, k // 32))).repeat(32)
    a = np.empty((k // 512, 16))
    for p in range(k // 512):
        a[p, :8] = np.random.permutation(np.resize(levels, 8))
        for g in range(8):
            far = levels[np.abs(levels - a[p, g]) >= 10]
            a[p, g + 8] = far[np.random.randint(len(far))]
    return np.exp2(a.ravel()).repeat(32)


def f64(x):
    return np.asarray(x).astype(np.float64)


def striped(idx):
    return np.tile(idx.reshape(-1, 16).T, (8, 1)).astype(np.uint16)


def unstriped(offs):
    return offs[:16].T.reshape(-1).astype(np.int64)


def striped8(idx):
    return np.concatenate([x.reshape(-1, 16).T for x in idx]).astype(np.uint16)


def runs(offs, k):
    lists = np.stack([offs[16 * r : 16 * r + 16].T.reshape(-1) for r in range(8)]).astype(np.int64)
    return lists[np.arange(k) % 512 // 64]


def pack_weight(w):
    k, n = w.shape
    w = f64(np.asarray(w, np.float32).astype(ml_dtypes.bfloat16)).reshape(k // 32, 32, n)
    amax = np.abs(w).max(1)
    byte = np.clip(np.where(amax > 0, np.frexp(amax)[1] - 1 + 127 - 7, 1), 1, 254)
    scaled = (w * np.exp2(127.0 - byte)[:, None, :]).reshape(k, n).astype(np.float32)
    words = np.ascontiguousarray(scaled.reshape(k // 512, 128, 4, n).transpose(0, 1, 3, 2)).astype(ml_dtypes.float8_e4m3fn).view(np.uint8)
    return words, np.ascontiguousarray(byte.astype(np.uint8).reshape(k // 512, 16, n))


def unpack_weight(words, scales):
    g, p, n, _ = words.shape
    vals = np.ascontiguousarray(words).view(ml_dtypes.float8_e4m3fn).astype(np.float64) * np.repeat(np.exp2(scales.astype(np.float64) - 127.0), 8, axis=1)[..., None]
    return vals.transpose(0, 1, 3, 2).reshape(g * 512, n)


def sigmoid(v):
    return 1.0 / (1.0 + np.exp(-np.maximum(v, -700.0)))

def planes(y):
    n, m = y.shape
    v = y.astype(np.float32).astype(ml_dtypes.bfloat16).astype(np.float64).reshape(n // 32, 32, m)
    top = np.abs(v).max(1)
    byte = np.clip(np.where(top > 0, np.frexp(top)[1] - 1 + 127 - 7, 1), 1, 254)
    codes = (v * np.exp2(127.0 - byte)[:, None, :]).reshape(n, m).astype(np.float32).astype(ml_dtypes.float8_e4m3fn).view(np.uint8)
    words = codes.reshape(n // 512, 128, 4, m).transpose(0, 1, 3, 2)
    return np.ascontiguousarray(words), np.ascontiguousarray(byte.astype(np.uint8).reshape(n // 512, 16, m))


K, T, S, H, C = 512, 2048, 512, 512, 512


def setup_inputs():
    n = np.random.standard_normal
    s = mx_kscale(K)[:, None]
    packed_xT = pack_weight(n((K, T)) * s)
    packed_w1 = pack_weight(n((K, H)) / np.sqrt(K) / s)
    packed_w2 = pack_weight(n((K, H)) / np.sqrt(K) / s)
    return {
        "x_words": packed_xT[0],
        "x_scales": packed_xT[1],
        "w1_words": packed_w1[0],
        "w1_scales": packed_w1[1],
        "w2_words": packed_w2[0],
        "w2_scales": packed_w2[1],
        "gs": (np.random.uniform(0.5, 1.5, (K, 1)) / s).astype(np.float32),
        "offs": striped(np.random.permutation(T)[:S]),
        "two": striped(np.random.permutation(T)[:S]),
        "n1": striped8(np.stack([np.random.permutation(S) for _ in range(8)])),
        "n2": striped8(np.stack([np.random.permutation(S) for _ in range(8)])),
        "n3": striped8(np.stack([np.random.permutation(S) for _ in range(8)])),
        "cand": striped(np.random.permutation(T)[:C]),
        "n4": striped8(np.stack([np.random.permutation(S) for _ in range(8)])),
        "n5": striped8(np.stack([np.random.permutation(S) for _ in range(8)])),
    }


def reference(x_words, x_scales, w1_words, w1_scales, w2_words, w2_scales, gs, offs, two, n1, n2, n3, cand, n4, n5):
    x_cand = unpack_weight(x_words, x_scales)[:, unstriped(cand)]
    xq = unpack_weight(x_words, x_scales)[:, unstriped(offs)]
    y = unpack_weight(w1_words, w1_scales).T @ xq
    x_two = unpack_weight(x_words, x_scales)[:, unstriped(two)]
    d = unpack_weight(w2_words, w2_scales).T @ x_two
    z = f64(gs) * (np.maximum(np.minimum(y - (0.5 * (y[np.arange(H)[:, None], runs(n1, H)])), d[np.arange(H)[:, None], runs(n2, H)]), d[np.arange(H)[:, None], runs(n3, H)]))
    s = 0.0625 * ((x_cand.T @ mxq(z, 0, "e4m3")))
    st = s * (sigmoid(s[np.arange(C)[:, None], runs(n4, C)]))
    out_0 = st - (st[np.arange(C)[:, None], runs(n5, C)])
    return (out_0,) + planes(out_0)

@@ -1,0 +1,264 @@
+from contextlib import ExitStack
+
+import concourse.mybir as mybir
+
+K, T, S = 512, 2048, 512
+FLOPS = 3 * 2 * K * S * S
+
+F32 = mybir.dt.float32
+BF16 = mybir.dt.bfloat16
+I32 = mybir.dt.int32
+U32 = mybir.dt.uint32
+U16 = mybir.dt.uint16
+U8 = mybir.dt.uint8
+FP8X4 = mybir.dt.float8_e4m3fn_x4
+ALU = mybir.AluOpType
+ACT = mybir.ActivationFunctionType
+
+P = 128
+PACK = 4
+HALF = S // 2
+QUARTER = S // 4
+
+
+def tile_picked_twcclampbhopg_none_po_kernel(
+    tc, x_words, x_scales, w1_words, w1_scales, w2_words, w2_scales, gs,
+    offs, two, n1, n2, n3, cand, n4, n5, out_0, out_1, out_2,
+):
+    nc = tc.nc
+    with ExitStack() as ctx:
+        keep = ctx.enter_context(tc.tile_pool(name="keep", bufs=1))
+        psum = ctx.enter_context(tc.psum_pool(name="psum", bufs=1))
+
+        def sb(name, shape, dtype, tag=None):
+            return keep.tile(shape, dtype, name=name, tag=tag or name, align_bytes=64)
+
+        def load_list(name, src):
+            tile = sb(name, [P, S // 16], U16)
+            nc.sync.dma_start(tile[:], src)
+            return tile
+
+        def load_words(name, src, width):
+            tile = sb(name, [P, width], I32)
+            nc.sync.dma_start(tile[:], src[0].rearrange("p n t -> p (n t)").bitcast(I32))
+            return tile
+
+        def entries(lst, start, count):
+            return lst[:, start // 16 : (start + count) // 16]
+
+        def deal(dst, src, run):
+            nc.vector.tensor_copy(
+                dst.rearrange("p (t c i) -> p c t i", t=PACK, i=run),
+                src.rearrange("p (c i t) -> p c t i", t=PACK, i=run),
+            )
+
+        def load_scales(name, src, width, queue):
+            tile = sb(name, [P, width], U8)
+            for q in range(4):
+                rows = src[0, 4 * q : 4 * q + 4, :].bitcast(I32)
+                queue.dma_start(
+                    tile[32 * q : 32 * q + 32, :].bitcast(I32),
+                    rows.unsqueeze(0).to_broadcast([8, 4, width // 4]),
+                )
+            return tile
+
+        x_sc = load_scales("x_sc", x_scales, T, nc.sync)
+        l_offs = load_list("l_offs", offs)
+        l_two = load_list("l_two", two)
+        x_w = load_words("x_w", x_words, T)
+        w1_raw = load_words("w1_raw", w1_words, S)
+        w1_sc_raw = load_scales("w1_sc_raw", w1_scales, S, nc.sync)
+        l_cand = load_list("l_cand", cand)
+        w2_raw = load_words("w2_raw", w2_words, S)
+        w2_sc_raw = load_scales("w2_sc_raw", w2_scales, S, nc.sync)
+        zero = sb("zero", [P, 1], F32)
+        nc.vector.memset(zero[:], 0.0)
+        l_n1 = load_list("l_n1", n1)
+        l_n2 = load_list("l_n2", n2)
+        l_n3 = load_list("l_n3", n3)
+        gain = sb("gain", [P, PACK], F32)
+        nc.sync.dma_start(gain[:], gs.rearrange("(p t) o -> p (t o)", t=PACK))
+        l_n4 = load_list("l_n4", n4)
+        l_n5 = load_list("l_n5", n5)
+
+        win_a = [sb("win_a%d" % t, [P, 2 * S], F32) for t in range(PACK)]
+        win_d = [sb("win_d%d" % t, [P, 2 * S], F32) for t in range(PACK)]
+        for t in range(PACK):
+            nc.scalar.activation(win_a[t][:, S:], zero[:].to_broadcast([P, S]), ACT.Sigmoid)
+
+        def pick_scales(name, lst):
+            tile = sb(name, [P, S], U8)
+            nc.vector.tensor_copy(tile[:], x_sc[:].indirect(lst[:]))
+            return tile
+
+        def pick_words(name, lst, tag=None):
+            tile = sb(name, [P, S], U32, tag)
+            nc.vector.tensor_copy(tile[:], x_w[:].bitcast(U32).indirect(lst[:]))
+            return tile
+
+        q_sc = pick_scales("q_sc", l_offs)
+        two_sc = pick_scales("two_sc", l_two)
+        q_w = pick_words("q_w", l_offs)
+        w1_w = sb("w1_w", [P, S], I32)
+        deal(w1_w[:], w1_raw[:], 4)
+        w1_sc = sb("w1_sc", [P, S], U8)
+        deal(w1_sc[:], w1_sc_raw[:], 16)
+
+        def product(tag, t, lhs_w, lhs_sc, k, rhs_w, rhs_sc):
+            bank = psum.tile([P, S], F32, name=tag, tag=tag)
+            cols = slice(t * P, (t + 1) * P)
+            nc.tensor.matmul_mx(
+                out=bank[:], lhsT=lhs_w[:, cols].bitcast(FP8X4), lhsT_scale=lhs_sc[k:P, cols],
+                rhs=rhs_w[:].bitcast(FP8X4), rhs_scale=rhs_sc[:], start=True, stop=True,
+            )
+            return bank
+
+        for t in range(PACK):
+            bank = product("bank%d" % t, t, w1_w, w1_sc, 0, q_w, q_sc)
+            nc.scalar.activation(win_a[t][:, :S], bank[:], ACT.Copy, scale=-0.5)
+            nc.scalar.copy(win_d[t][:, S:], bank[:])
+
+        two_w = pick_words("two_w", l_two)
+        w2_w = sb("w2_w", [P, S], I32)
+        deal(w2_w[:], w2_raw[:], 4)
+        w2_sc = sb("w2_sc", [P, S], U8)
+        deal(w2_sc[:], w2_sc_raw[:], 16)
+        cand_sc_raw = pick_scales("cand_sc_raw", l_cand)
+        cand_sc = sb("cand_sc", [P, S], U8)
+        deal(cand_sc[:], cand_sc_raw[:], 16)
+        for t in range(PACK):
+            bank = product("bank%d" % (PACK + t), t, w2_w, w2_sc, 0, two_w, two_sc)
+            nc.scalar.copy(win_d[t][:, :S], bank[:])
+
+        a = [sb("a%d" % t, [P, S], F32) for t in range(PACK)]
+        for t in range(PACK):
+            nc.vector.tensor_tensor(a[t][:], win_a[t][:].indirect(l_n1[:]), win_d[t][:, S:], ALU.add)
+
+        z_bf = [sb("z_bf%d" % h, [P, HALF, PACK], BF16) for h in range(2)]
+        z_w = sb("z_w", [P, S], U32)
+        z_sc = sb("z_sc", [P, S], U8)
+
+        def quantize(words, scales, start, src):
+            width = src.shape[1]
+            nc.vector.quantize_mx(
+                out=words[:, start : start + width].bitcast(FP8X4),
+                scales=scales[:, start : start + width],
+                in_=src[:].rearrange("p c t -> p (c t)"),
+            )
+
+        pieces = [(0, 0, S), (1, 0, S), (2, 0, S), (3, 0, HALF), (3, HALF, HALF)]
+        low, high = [], []
+
+        def fetch(n, lst, store, kind):
+            t, start, count = pieces[n]
+            last = n == len(pieces) - 1 and kind == "high"
+            tile = sb("%s%d" % (kind, n), [P, count], F32, "late" if last else None)
+            nc.vector.tensor_copy(tile[:], win_d[t][:].indirect(entries(lst, start, count)))
+            store.append(tile)
+
+        def take_min(n):
+            t, start, count = pieces[n]
+            nc.vector.tensor_tensor(low[n][:], low[n][:], a[t][:, start : start + count], ALU.min)
+
+        def take_max(n):
+            t, start, count = pieces[n]
+            nc.vector.tensor_tensor(low[n][:], low[n][:], high[n][:], ALU.max)
+            for h in range(start // HALF, (start + count) // HALF):
+                nc.scalar.activation(
+                    z_bf[h][:, :, t], low[n][:, h * HALF - start : (h + 1) * HALF - start],
+                    ACT.Copy, scale=gain[:, t : t + 1],
+                )
+
+        fetch(0, l_n2, low, "low")
+        for n in range(len(pieces)):
+            fetch(n, l_n3, high, "high")
+            take_min(n)
+            if n + 1 < len(pieces):
+                fetch(n + 1, l_n2, low, "low")
+            else:
+                quantize(z_w, z_sc, 0, z_bf[0])
+            take_max(n)
+
+        cand_raw = pick_words("cand_raw", l_cand, "late")
+        quantize(z_w, z_sc, HALF, z_bf[1])
+        cand_w = sb("cand_w", [P, S], I32)
+        deal(cand_w[:], cand_raw[:].bitcast(I32), 4)
+
+        banks = [product("bank%d" % t, t, cand_w, cand_sc, 0, z_w, z_sc) for t in range(PACK)]
+        neg = [sb("neg%d" % t, [P, S], F32) for t in range(PACK)]
+        neg_copy = [sb("neg_copy%d" % t, [P, S], F32) for t in range(PACK)]
+        other = [sb("other%d" % t, [P, S], F32) for t in range(PACK)]
+        res = [sb("res%d" % h, [P, PACK, HALF], F32) for h in range(2)]
+        out_rows = out_0.rearrange("(p t) j -> p t j", t=PACK)
+
+        def gate(t):
+            nc.scalar.activation(win_a[t][:, :S], banks[t][:], ACT.Copy, scale=0.0625)
+            nc.scalar.activation(other[t][:], win_a[t][:].indirect(l_n4[:]), ACT.Sigmoid)
+
+        def gated(t):
+            nc.vector.scalar_tensor_tensor(neg[t][:], banks[t][:], -0.0625, other[t][:], ALU.mult, ALU.mult)
+
+        def duplicate(t, copy):
+            copy(neg_copy[t][:], neg[t][:])
+
+        def differ(t, h):
+            cols = slice(h * HALF, (h + 1) * HALF)
+            nc.vector.tensor_tensor(
+                res[h][:, t, :], neg[t][:].indirect(entries(l_n5, h * HALF, HALF)), neg_copy[t][:, cols], ALU.subtract
+            )
+
+        def store(h, t0, t1):
+            nc.sync.dma_start(out_rows[:, t0:t1, h * HALF : (h + 1) * HALF], res[h][:, t0:t1, :])
+
+        nc.scalar.activation(win_a[0][:, :S], banks[0][:], ACT.Sigmoid, scale=0.0625)
+        nc.vector.tensor_scalar(other[0][:], banks[0][:], -0.0625, None, ALU.mult)
+        nc.vector.tensor_tensor(neg[0][:], win_a[0][:].indirect(l_n4[:]), other[0][:], ALU.mult)
+        gate(1)
+        duplicate(0, nc.vector.tensor_copy)
+        gated(1)
+        differ(0, 0)
+        differ(0, 1)
+        gate(2)
+        duplicate(1, nc.vector.tensor_copy)
+        gated(2)
+        differ(1, 0)
+        differ(1, 1)
+        store(0, 0, 2)
+        store(1, 0, 2)
+        gate(3)
+        gated(3)
+        duplicate(2, nc.scalar.copy)
+        duplicate(3, nc.scalar.copy)
+        differ(2, 0)
+        differ(3, 0)
+        store(0, 2, 4)
+
+        o_w = sb("o_w", [P, S], U32)
+        o_sc = sb("o_sc", [P, S], U8)
+
+        def interleave(copy, name, h, start, count):
+            tile = sb(name, [P, count, PACK], BF16)
+            copy(
+                tile[:].rearrange("p (c i) t -> p c t i", i=4),
+                res[h][:, :, start : start + count].rearrange("p t (c i) -> p c t i", i=4),
+            )
+            return tile
+
+        words_out = out_1[0].rearrange("p n t -> p (n t)").bitcast(I32)
+        o_first = interleave(nc.scalar.copy, "o_first", 0, 0, HALF)
+        differ(2, 1)
+        store(1, 2, 3)
+        differ(3, 1)
+        store(1, 3, 4)
+        o_last = interleave(nc.scalar.copy, "o_last", 1, QUARTER, QUARTER)
+        o_mid = interleave(nc.vector.tensor_copy, "o_mid", 1, 0, QUARTER)
+        quantize(o_w, o_sc, 0, o_first)
+        nc.sync.dma_start(words_out[:, :HALF], o_w[:, :HALF].bitcast(I32))
+        quantize(o_w, o_sc, HALF, o_mid)
+        quantize(o_w, o_sc, HALF + QUARTER, o_last)
+        nc.sync.dma_start(words_out[:, HALF:], o_w[:, HALF:].bitcast(I32))
+        for q in range(4):
+            queue = nc.scalar if q % 2 else nc.sync
+            queue.dma_start(
+                out_2[0, 4 * q : 4 * q + 4, :].bitcast(I32), o_sc[32 * q : 32 * q + 4, :].bitcast(I32)
+            )

@@ -1,6 +1,7 @@
 from contextlib import ExitStack
 
 import concourse.mybir as mybir
+from concourse.masks import make_identity
 
 K, T, S = 512, 2048, 512
 FLOPS = 3 * 2 * K * S * S
@@ -52,27 +53,34 @@ def tile_picked_twcclampbhopg_none_po_kernel(
                 src.rearrange("p (c i t) -> p c t i", t=PACK, i=run),
             )
 
-        def load_scales(name, src, width, queue):
+        def deal_weights(dst, src):
+            nc.gpsimd.tensor_copy(
+                dst.rearrange("p (t m) -> p t m", t=PACK), src.rearrange("p (m t) -> p t m", t=PACK)
+            )
+
+        def load_scales(name, src, width, queues):
             tile = sb(name, [P, width], U8)
             for q in range(4):
                 rows = src[0, 4 * q : 4 * q + 4, :].bitcast(I32)
-                queue.dma_start(
+                queues[q % len(queues)].dma_start(
                     tile[32 * q : 32 * q + 32, :].bitcast(I32),
                     rows.unsqueeze(0).to_broadcast([8, 4, width // 4]),
                 )
             return tile
 
-        x_sc = load_scales("x_sc", x_scales, T, nc.sync)
         l_offs = load_list("l_offs", offs)
+        x_sc = load_scales("x_sc", x_scales, T, [nc.scalar, nc.sync])
         l_two = load_list("l_two", two)
         x_w = load_words("x_w", x_words, T)
         w1_raw = load_words("w1_raw", w1_words, S)
-        w1_sc_raw = load_scales("w1_sc_raw", w1_scales, S, nc.sync)
+        w1_sc_raw = load_scales("w1_sc_raw", w1_scales, S, [nc.sync])
         l_cand = load_list("l_cand", cand)
         w2_raw = load_words("w2_raw", w2_words, S)
-        w2_sc_raw = load_scales("w2_sc_raw", w2_scales, S, nc.sync)
+        w2_sc_raw = load_scales("w2_sc_raw", w2_scales, S, [nc.sync])
         zero = sb("zero", [P, 1], F32)
         nc.vector.memset(zero[:], 0.0)
+        ident = sb("ident", [P, P], F32)
+        make_identity(nc, ident[:])
         l_n1 = load_list("l_n1", n1)
         l_n2 = load_list("l_n2", n2)
         l_n3 = load_list("l_n3", n3)
@@ -100,9 +108,9 @@ def tile_picked_twcclampbhopg_none_po_kernel(
         two_sc = pick_scales("two_sc", l_two)
         q_w = pick_words("q_w", l_offs)
         w1_w = sb("w1_w", [P, S], I32)
-        deal(w1_w[:], w1_raw[:], 4)
+        deal_weights(w1_w[:], w1_raw[:])
         w1_sc = sb("w1_sc", [P, S], U8)
-        deal(w1_sc[:], w1_sc_raw[:], 16)
+        deal_weights(w1_sc[:], w1_sc_raw[:])
 
         def product(tag, t, lhs_w, lhs_sc, k, rhs_w, rhs_sc):
             bank = psum.tile([P, S], F32, name=tag, tag=tag)
@@ -120,12 +128,10 @@ def tile_picked_twcclampbhopg_none_po_kernel(
 
         two_w = pick_words("two_w", l_two)
         w2_w = sb("w2_w", [P, S], I32)
-        deal(w2_w[:], w2_raw[:], 4)
+        deal_weights(w2_w[:], w2_raw[:])
         w2_sc = sb("w2_sc", [P, S], U8)
-        deal(w2_sc[:], w2_sc_raw[:], 16)
+        deal_weights(w2_sc[:], w2_sc_raw[:])
         cand_sc_raw = pick_scales("cand_sc_raw", l_cand)
-        cand_sc = sb("cand_sc", [P, S], U8)
-        deal(cand_sc[:], cand_sc_raw[:], 16)
         for t in range(PACK):
             bank = product("bank%d" % (PACK + t), t, w2_w, w2_sc, 0, two_w, two_sc)
             nc.scalar.copy(win_d[t][:, :S], bank[:])
@@ -146,43 +152,76 @@ def tile_picked_twcclampbhopg_none_po_kernel(
                 in_=src[:].rearrange("p c t -> p (c t)"),
             )
 
-        pieces = [(0, 0, S), (1, 0, S), (2, 0, S), (3, 0, HALF), (3, HALF, HALF)]
-        low, high = [], []
+        def write_z(t, h, src):
+            nc.scalar.activation(z_bf[h][:, :, t], src, ACT.Copy, scale=gain[:, t : t + 1])
 
-        def fetch(n, lst, store, kind):
-            t, start, count = pieces[n]
-            last = n == len(pieces) - 1 and kind == "high"
-            tile = sb("%s%d" % (kind, n), [P, count], F32, "late" if last else None)
-            nc.vector.tensor_copy(tile[:], win_d[t][:].indirect(entries(lst, start, count)))
-            store.append(tile)
+        low = [sb("low%d" % t, [P, S], F32) for t in range(PACK - 1)]
+        high = [sb("high%d" % t, [P, S], F32) for t in range(PACK - 1)]
 
-        def take_min(n):
-            t, start, count = pieces[n]
-            nc.vector.tensor_tensor(low[n][:], low[n][:], a[t][:, start : start + count], ALU.min)
+        def fetch_less_a(t, lst, dst):
+            nc.vector.tensor_tensor(dst[t][:], win_d[t][:].indirect(lst[:]), a[t][:], ALU.subtract)
 
-        def take_max(n):
-            t, start, count = pieces[n]
-            nc.vector.tensor_tensor(low[n][:], low[n][:], high[n][:], ALU.max)
-            for h in range(start // HALF, (start + count) // HALF):
-                nc.scalar.activation(
-                    z_bf[h][:, :, t], low[n][:, h * HALF - start : (h + 1) * HALF - start],
-                    ACT.Copy, scale=gain[:, t : t + 1],
-                )
+        def clamp(t):
+            nc.vector.scalar_tensor_tensor(low[t][:], low[t][:], 0.0, high[t][:], ALU.min, ALU.max)
+            first, second = (4, 6) if t % 2 == 0 else (6, 4)
+            turned = []
+            for h in range(2):
+                bank = psum.tile([P, 2, P], F32, name="sum", tag="bank%d" % (first + h))
+                for b in range(2):
+                    cols = slice(h * HALF + b * P, h * HALF + (b + 1) * P)
+                    nc.tensor.matmul(bank[:, b, :], a[t][:, cols], ident[:], start=True, stop=False, is_transpose=True)
+                    nc.tensor.matmul(bank[:, b, :], low[t][:, cols], ident[:], start=False, stop=True, is_transpose=True)
+                tile = sb("turned%d_%d" % (t, h), [P, 2, P], F32)
+                nc.scalar.copy(tile[:], bank[:])
+                turned.append(tile)
+            for h in range(2):
+                bank = psum.tile([P, HALF], F32, name="back", tag="bank%d" % (second + h))
+                for b in range(2):
+                    nc.tensor.transpose(bank[:, b * P : (b + 1) * P], turned[h][:, b, :], ident[:])
+                write_z(t, h, bank[:])
 
-        fetch(0, l_n2, low, "low")
-        for n in range(len(pieces)):
-            fetch(n, l_n3, high, "high")
-            take_min(n)
-            if n + 1 < len(pieces):
-                fetch(n + 1, l_n2, low, "low")
-            else:
-                quantize(z_w, z_sc, 0, z_bf[0])
-            take_max(n)
+        last = PACK - 1
+        low_l = [sb("low_l%d" % h, [P, HALF], F32) for h in range(2)]
+        high_l = [sb("high_l0", [P, HALF], F32), sb("high_l1", [P, HALF], F32, "late")]
+
+        def fetch_last(h, lst, dst):
+            nc.vector.tensor_copy(dst[h][:], win_d[last][:].indirect(entries(lst, h * HALF, HALF)))
+
+        def min_last(h):
+            nc.vector.tensor_tensor(low_l[h][:], low_l[h][:], a[last][:, h * HALF : (h + 1) * HALF], ALU.min)
+
+        def max_last(h):
+            nc.vector.tensor_tensor(low_l[h][:], low_l[h][:], high_l[h][:], ALU.max)
+            write_z(last, h, low_l[h][:])
+
+        fetch_less_a(0, l_n2, low)
+        fetch_less_a(0, l_n3, high)
+        fetch_less_a(1, l_n2, low)
+        clamp(0)
+        fetch_less_a(1, l_n3, high)
+        nc.vector.tensor_copy(low[2][:], win_d[2][:].indirect(l_n2[:]))
+        clamp(1)
+        nc.vector.tensor_copy(high[2][:], win_d[2][:].indirect(l_n3[:]))
+        nc.vector.tensor_tensor(low[2][:], low[2][:], a[2][:], ALU.min)
+        fetch_last(0, l_n2, low_l)
+        nc.vector.tensor_tensor(low[2][:], low[2][:], high[2][:], ALU.max)
+        for h in range(2):
+            write_z(2, h, low[2][:, h * HALF : (h + 1) * HALF])
+        fetch_last(0, l_n3, high_l)
+        min_last(0)
+        fetch_last(1, l_n2, low_l)
+        max_last(0)
+        fetch_last(1, l_n3, high_l)
+        min_last(1)
+        cand_sc = sb("cand_sc", [P, S], U8)
+        deal(cand_sc[:], cand_sc_raw[:], 16)
+        max_last(1)
 
         cand_raw = pick_words("cand_raw", l_cand, "late")
-        quantize(z_w, z_sc, HALF, z_bf[1])
+        quantize(z_w, z_sc, 0, z_bf[0])
         cand_w = sb("cand_w", [P, S], I32)
         deal(cand_w[:], cand_raw[:].bitcast(I32), 4)
+        quantize(z_w, z_sc, HALF, z_bf[1])
 
         banks = [product("bank%d" % t, t, cand_w, cand_sc, 0, z_w, z_sc) for t in range(PACK)]
         neg = [sb("neg%d" % t, [P, S], F32) for t in range(PACK)]

@@ -136,9 +136,14 @@ def tile_picked_twcclampbhopg_none_po_kernel(
             bank = product("bank%d" % (PACK + t), t, w2_w, w2_sc, 0, two_w, two_sc)
             nc.scalar.copy(win_d[t][:, :S], bank[:])
 
-        a = [sb("a%d" % t, [P, S], F32) for t in range(PACK)]
-        for t in range(PACK):
+        a = {}
+
+        def fetch_a(t, tag=None):
+            a[t] = sb("a%d" % t, [P, S], F32, tag)
             nc.vector.tensor_tensor(a[t][:], win_a[t][:].indirect(l_n1[:]), win_d[t][:, S:], ALU.add)
+
+        for t in range(PACK - 1):
+            fetch_a(t)
 
         z_bf = [sb("z_bf%d" % h, [P, HALF, PACK], BF16) for h in range(2)]
         z_w = sb("z_w", [P, S], U32)
@@ -163,7 +168,7 @@ def tile_picked_twcclampbhopg_none_po_kernel(
 
         def clamp(t):
             nc.vector.scalar_tensor_tensor(low[t][:], low[t][:], 0.0, high[t][:], ALU.min, ALU.max)
-            first, second = (4, 6) if t % 2 == 0 else (6, 4)
+            first, second = (4, 6) if t == 0 else (0, 2)
             turned = []
             for h in range(2):
                 bank = psum.tile([P, 2, P], F32, name="sum", tag="bank%d" % (first + h))
@@ -181,18 +186,16 @@ def tile_picked_twcclampbhopg_none_po_kernel(
                 write_z(t, h, bank[:])
 
         last = PACK - 1
-        low_l = [sb("low_l%d" % h, [P, HALF], F32) for h in range(2)]
+        low_l = sb("low_l", [P, S], F32)
         high_l = [sb("high_l0", [P, HALF], F32), sb("high_l1", [P, HALF], F32, "late")]
 
-        def fetch_last(h, lst, dst):
-            nc.vector.tensor_copy(dst[h][:], win_d[last][:].indirect(entries(lst, h * HALF, HALF)))
-
-        def min_last(h):
-            nc.vector.tensor_tensor(low_l[h][:], low_l[h][:], a[last][:, h * HALF : (h + 1) * HALF], ALU.min)
+        def fetch_high_last(h):
+            nc.vector.tensor_copy(high_l[h][:], win_d[last][:].indirect(entries(l_n3, h * HALF, HALF)))
 
         def max_last(h):
-            nc.vector.tensor_tensor(low_l[h][:], low_l[h][:], high_l[h][:], ALU.max)
-            write_z(last, h, low_l[h][:])
+            part = low_l[:, h * HALF : (h + 1) * HALF]
+            nc.vector.tensor_tensor(part, part, high_l[h][:], ALU.max)
+            write_z(last, h, part)
 
         fetch_less_a(0, l_n2, low)
         fetch_less_a(0, l_n3, high)
@@ -203,31 +206,39 @@ def tile_picked_twcclampbhopg_none_po_kernel(
         clamp(1)
         nc.vector.tensor_copy(high[2][:], win_d[2][:].indirect(l_n3[:]))
         nc.vector.tensor_tensor(low[2][:], low[2][:], a[2][:], ALU.min)
-        fetch_last(0, l_n2, low_l)
+        fetch_a(last, "high1")
         nc.vector.tensor_tensor(low[2][:], low[2][:], high[2][:], ALU.max)
         for h in range(2):
             write_z(2, h, low[2][:, h * HALF : (h + 1) * HALF])
-        fetch_last(0, l_n3, high_l)
-        min_last(0)
-        fetch_last(1, l_n2, low_l)
+        nc.vector.tensor_copy(low_l[:], win_d[last][:].indirect(l_n2[:]))
+        fetch_high_last(0)
+        nc.vector.tensor_tensor(low_l[:], low_l[:], a[last][:], ALU.min)
+        fetch_high_last(1)
         max_last(0)
-        fetch_last(1, l_n3, high_l)
-        min_last(1)
         cand_sc = sb("cand_sc", [P, S], U8)
         deal(cand_sc[:], cand_sc_raw[:], 16)
         max_last(1)
 
-        cand_raw = pick_words("cand_raw", l_cand, "late")
+        cand_w = sb("cand_w", [P, S], U32, "late")
+        nc.vector.tensor_copy(
+            cand_w[:].rearrange("p (t m) -> p m t", t=PACK), x_w[:].bitcast(U32).indirect(l_cand[:])
+        )
         quantize(z_w, z_sc, 0, z_bf[0])
-        cand_w = sb("cand_w", [P, S], I32)
-        deal(cand_w[:], cand_raw[:].bitcast(I32), 4)
         quantize(z_w, z_sc, HALF, z_bf[1])
 
-        banks = [product("bank%d" % t, t, cand_w, cand_sc, 0, z_w, z_sc) for t in range(PACK)]
-        neg = [sb("neg%d" % t, [P, S], F32) for t in range(PACK)]
+        first_halves = []
+        for h in range(2):
+            bank = psum.tile([P, HALF], F32, name="first_half", tag="bank%d" % (PACK * h))
+            cols = slice(h * HALF, (h + 1) * HALF)
+            nc.tensor.matmul_mx(
+                out=bank[:], lhsT=cand_w[:, :P].bitcast(FP8X4), lhsT_scale=cand_sc[:, :P],
+                rhs=z_w[:, cols].bitcast(FP8X4), rhs_scale=z_sc[:, cols], start=True, stop=True,
+            )
+            first_halves.append(bank)
+        banks = {t: product("bank%d" % t, t, cand_w, cand_sc, 0, z_w, z_sc) for t in range(1, PACK)}
         neg_copy = [sb("neg_copy%d" % t, [P, S], F32) for t in range(PACK)]
         other = [sb("other%d" % t, [P, S], F32) for t in range(PACK)]
-        res = [sb("res%d" % h, [P, PACK, HALF], F32) for h in range(2)]
+        res = sb("res", [P, PACK, S], F32)
         out_rows = out_0.rearrange("(p t) j -> p t j", t=PACK)
 
         def gate(t):
@@ -235,62 +246,62 @@ def tile_picked_twcclampbhopg_none_po_kernel(
             nc.scalar.activation(other[t][:], win_a[t][:].indirect(l_n4[:]), ACT.Sigmoid)
 
         def gated(t):
-            nc.vector.scalar_tensor_tensor(neg[t][:], banks[t][:], -0.0625, other[t][:], ALU.mult, ALU.mult)
+            nc.vector.scalar_tensor_tensor(win_d[t][:, :S], banks[t][:], -0.0625, other[t][:], ALU.mult, ALU.mult)
 
         def duplicate(t, copy):
-            copy(neg_copy[t][:], neg[t][:])
+            copy(neg_copy[t][:], win_d[t][:, :S])
 
-        def differ(t, h):
-            cols = slice(h * HALF, (h + 1) * HALF)
+        def differ(t, start, count):
+            cols = slice(start, start + count)
             nc.vector.tensor_tensor(
-                res[h][:, t, :], neg[t][:].indirect(entries(l_n5, h * HALF, HALF)), neg_copy[t][:, cols], ALU.subtract
+                res[:, t, cols], win_d[t][:].indirect(entries(l_n5, start, count)), neg_copy[t][:, cols], ALU.subtract
             )
 
-        def store(h, t0, t1):
-            nc.sync.dma_start(out_rows[:, t0:t1, h * HALF : (h + 1) * HALF], res[h][:, t0:t1, :])
+        def store(t0, t1, start, count):
+            cols = slice(start, start + count)
+            nc.sync.dma_start(out_rows[:, t0:t1, cols], res[:, t0:t1, cols])
 
-        nc.scalar.activation(win_a[0][:, :S], banks[0][:], ACT.Sigmoid, scale=0.0625)
-        nc.vector.tensor_scalar(other[0][:], banks[0][:], -0.0625, None, ALU.mult)
-        nc.vector.tensor_tensor(neg[0][:], win_a[0][:].indirect(l_n4[:]), other[0][:], ALU.mult)
+        for h in range(2):
+            cols = slice(h * HALF, (h + 1) * HALF)
+            nc.scalar.activation(win_a[0][:, cols], first_halves[h][:], ACT.Sigmoid, scale=0.0625)
+            nc.vector.tensor_scalar(other[0][:, cols], first_halves[h][:], -0.0625, None, ALU.mult)
+        nc.vector.tensor_tensor(win_d[0][:, :S], win_a[0][:].indirect(l_n4[:]), other[0][:], ALU.mult)
         gate(1)
-        duplicate(0, nc.vector.tensor_copy)
+        duplicate(0, nc.gpsimd.tensor_copy)
         gated(1)
-        differ(0, 0)
-        differ(0, 1)
+        differ(0, 0, S)
+        store(0, 1, 0, S)
         gate(2)
-        duplicate(1, nc.vector.tensor_copy)
+        duplicate(1, nc.gpsimd.tensor_copy)
         gated(2)
-        differ(1, 0)
-        differ(1, 1)
-        store(0, 0, 2)
-        store(1, 0, 2)
+        differ(1, 0, S)
+        store(1, 2, 0, S)
         gate(3)
         gated(3)
         duplicate(2, nc.scalar.copy)
         duplicate(3, nc.scalar.copy)
-        differ(2, 0)
-        differ(3, 0)
-        store(0, 2, 4)
+        differ(2, 0, HALF)
+        differ(3, 0, HALF)
+        store(2, 4, 0, HALF)
 
         o_w = sb("o_w", [P, S], U32)
         o_sc = sb("o_sc", [P, S], U8)
 
-        def interleave(copy, name, h, start, count):
+        def interleave(copy, name, start, count):
             tile = sb(name, [P, count, PACK], BF16)
             copy(
                 tile[:].rearrange("p (c i) t -> p c t i", i=4),
-                res[h][:, :, start : start + count].rearrange("p t (c i) -> p c t i", i=4),
+                res[:, :, start : start + count].rearrange("p t (c i) -> p c t i", i=4),
             )
             return tile
 
         words_out = out_1[0].rearrange("p n t -> p (n t)").bitcast(I32)
-        o_first = interleave(nc.scalar.copy, "o_first", 0, 0, HALF)
-        differ(2, 1)
-        store(1, 2, 3)
-        differ(3, 1)
-        store(1, 3, 4)
-        o_last = interleave(nc.scalar.copy, "o_last", 1, QUARTER, QUARTER)
-        o_mid = interleave(nc.vector.tensor_copy, "o_mid", 1, 0, QUARTER)
+        o_first = interleave(nc.scalar.copy, "o_first", 0, HALF)
+        differ(2, HALF, HALF)
+        differ(3, HALF, HALF)
+        store(2, 4, HALF, HALF)
+        o_last = interleave(nc.scalar.copy, "o_last", HALF + QUARTER, QUARTER)
+        o_mid = interleave(nc.vector.tensor_copy, "o_mid", HALF, QUARTER)
         quantize(o_w, o_sc, 0, o_first)
         nc.sync.dma_start(words_out[:, :HALF], o_w[:, :HALF].bitcast(I32))
         quantize(o_w, o_sc, HALF, o_mid)

@@ -18,8 +18,13 @@ ACT = mybir.ActivationFunctionType
 
 P = 128
 PACK = 4
+QUADRANTS = 4
+GROUP = 16
+LINE = 16
 HALF = S // 2
 QUARTER = S // 4
+SCORE_SCALE = 0.0625
+LAST = PACK - 1
 
 
 def tile_picked_twcclampbhopg_none_po_kernel(
@@ -34,8 +39,17 @@ def tile_picked_twcclampbhopg_none_po_kernel(
         def sb(name, shape, dtype, tag=None):
             return keep.tile(shape, dtype, name=name, tag=tag or name, align_bytes=64)
 
+        def psum_bank(number, shape):
+            return psum.tile(shape, F32, name="bank%d" % number, tag="bank%d" % number)
+
+        def half_cols(h):
+            return slice(h * HALF, (h + 1) * HALF)
+
+        def entries(lst, start, count):
+            return lst[:, start // GROUP : (start + count) // GROUP]
+
         def load_list(name, src):
-            tile = sb(name, [P, S // 16], U16)
+            tile = sb(name, [P, S // GROUP], U16)
             nc.sync.dma_start(tile[:], src)
             return tile
 
@@ -44,27 +58,14 @@ def tile_picked_twcclampbhopg_none_po_kernel(
             nc.sync.dma_start(tile[:], src[0].rearrange("p n t -> p (n t)").bitcast(I32))
             return tile
 
-        def entries(lst, start, count):
-            return lst[:, start // 16 : (start + count) // 16]
-
-        def deal(dst, src, run):
-            nc.vector.tensor_copy(
-                dst.rearrange("p (t c i) -> p c t i", t=PACK, i=run),
-                src.rearrange("p (c i t) -> p c t i", t=PACK, i=run),
-            )
-
-        def deal_weights(dst, src):
-            nc.gpsimd.tensor_copy(
-                dst.rearrange("p (t m) -> p t m", t=PACK), src.rearrange("p (m t) -> p t m", t=PACK)
-            )
-
         def load_scales(name, src, width, queues):
             tile = sb(name, [P, width], U8)
-            for q in range(4):
-                rows = src[0, 4 * q : 4 * q + 4, :].bitcast(I32)
+            repeats = P // QUADRANTS // PACK
+            for q in range(QUADRANTS):
+                rows = src[0, PACK * q : PACK * (q + 1), :].bitcast(I32)
                 queues[q % len(queues)].dma_start(
-                    tile[32 * q : 32 * q + 32, :].bitcast(I32),
-                    rows.unsqueeze(0).to_broadcast([8, 4, width // 4]),
+                    tile[32 * q : 32 * (q + 1), :].bitcast(I32),
+                    rows.unsqueeze(0).to_broadcast([repeats, PACK, width // 4]),
                 )
             return tile
 
@@ -89,60 +90,66 @@ def tile_picked_twcclampbhopg_none_po_kernel(
         l_n4 = load_list("l_n4", n4)
         l_n5 = load_list("l_n5", n5)
 
-        win_a = [sb("win_a%d" % t, [P, 2 * S], F32) for t in range(PACK)]
-        win_d = [sb("win_d%d" % t, [P, 2 * S], F32) for t in range(PACK)]
+        first_win = [sb("first_win%d" % t, [P, 2 * S], F32) for t in range(PACK)]
+        second_win = [sb("second_win%d" % t, [P, 2 * S], F32) for t in range(PACK)]
         for t in range(PACK):
-            nc.scalar.activation(win_a[t][:, S:], zero[:].to_broadcast([P, S]), ACT.Sigmoid)
+            nc.scalar.activation(first_win[t][:, S:], zero[:].to_broadcast([P, S]), ACT.Sigmoid)
 
         def pick_scales(name, lst):
             tile = sb(name, [P, S], U8)
             nc.vector.tensor_copy(tile[:], x_sc[:].indirect(lst[:]))
             return tile
 
-        def pick_words(name, lst, tag=None):
-            tile = sb(name, [P, S], U32, tag)
+        def pick_words(name, lst):
+            tile = sb(name, [P, S], U32)
             nc.vector.tensor_copy(tile[:], x_w[:].bitcast(U32).indirect(lst[:]))
             return tile
 
-        q_sc = pick_scales("q_sc", l_offs)
-        two_sc = pick_scales("two_sc", l_two)
-        q_w = pick_words("q_w", l_offs)
-        w1_w = sb("w1_w", [P, S], I32)
-        deal_weights(w1_w[:], w1_raw[:])
-        w1_sc = sb("w1_sc", [P, S], U8)
-        deal_weights(w1_sc[:], w1_sc_raw[:])
+        def deal_weights(dst, src, t0, t1):
+            nc.gpsimd.tensor_copy(
+                dst[:].rearrange("p (t m) -> p t m", t=PACK)[:, t0:t1, :],
+                src[:].rearrange("p (m t) -> p t m", t=PACK)[:, t0:t1, :],
+            )
 
-        def product(tag, t, lhs_w, lhs_sc, k, rhs_w, rhs_sc):
-            bank = psum.tile([P, S], F32, name=tag, tag=tag)
+        def product(bank_number, t, lhs_w, lhs_sc, rhs_w, rhs_sc):
+            bank = psum_bank(bank_number, [P, rhs_w.shape[1]])
             cols = slice(t * P, (t + 1) * P)
             nc.tensor.matmul_mx(
-                out=bank[:], lhsT=lhs_w[:, cols].bitcast(FP8X4), lhsT_scale=lhs_sc[k:P, cols],
-                rhs=rhs_w[:].bitcast(FP8X4), rhs_scale=rhs_sc[:], start=True, stop=True,
+                out=bank[:], lhsT=lhs_w[:, cols].bitcast(FP8X4), lhsT_scale=lhs_sc[:, cols],
+                rhs=rhs_w.bitcast(FP8X4), rhs_scale=rhs_sc, start=True, stop=True,
             )
             return bank
 
+        idx_sc = pick_scales("idx_sc", l_offs)
+        two_sc = pick_scales("two_sc", l_two)
+        idx_w = pick_words("idx_w", l_offs)
+        w1_w = sb("w1_w", [P, S], I32)
+        w1_sc = sb("w1_sc", [P, S], U8)
+        for t0, t1 in ((0, 1), (1, PACK)):
+            deal_weights(w1_w, w1_raw, t0, t1)
+            deal_weights(w1_sc, w1_sc_raw, t0, t1)
         for t in range(PACK):
-            bank = product("bank%d" % t, t, w1_w, w1_sc, 0, q_w, q_sc)
-            nc.scalar.activation(win_a[t][:, :S], bank[:], ACT.Copy, scale=-0.5)
-            nc.scalar.copy(win_d[t][:, S:], bank[:])
+            bank = product(t, t, w1_w, w1_sc, idx_w[:], idx_sc[:])
+            nc.scalar.activation(first_win[t][:, :S], bank[:], ACT.Copy, scale=-0.5)
+            nc.scalar.copy(second_win[t][:, S:], bank[:])
 
         two_w = pick_words("two_w", l_two)
         w2_w = sb("w2_w", [P, S], I32)
-        deal_weights(w2_w[:], w2_raw[:])
+        deal_weights(w2_w, w2_raw, 0, PACK)
         w2_sc = sb("w2_sc", [P, S], U8)
-        deal_weights(w2_sc[:], w2_sc_raw[:])
+        deal_weights(w2_sc, w2_sc_raw, 0, PACK)
         cand_sc_raw = pick_scales("cand_sc_raw", l_cand)
         for t in range(PACK):
-            bank = product("bank%d" % (PACK + t), t, w2_w, w2_sc, 0, two_w, two_sc)
-            nc.scalar.copy(win_d[t][:, :S], bank[:])
+            bank = product(PACK + t, t, w2_w, w2_sc, two_w[:], two_sc[:])
+            nc.scalar.copy(second_win[t][:, :S], bank[:])
 
         a = {}
 
         def fetch_a(t, tag=None):
             a[t] = sb("a%d" % t, [P, S], F32, tag)
-            nc.vector.tensor_tensor(a[t][:], win_a[t][:].indirect(l_n1[:]), win_d[t][:, S:], ALU.add)
+            nc.vector.tensor_tensor(a[t][:], first_win[t][:].indirect(l_n1[:]), second_win[t][:, S:], ALU.add)
 
-        for t in range(PACK - 1):
+        for t in range(LAST):
             fetch_a(t)
 
         z_bf = [sb("z_bf%d" % h, [P, HALF, PACK], BF16) for h in range(2)]
@@ -150,28 +157,27 @@ def tile_picked_twcclampbhopg_none_po_kernel(
         z_sc = sb("z_sc", [P, S], U8)
 
         def quantize(words, scales, start, src):
-            width = src.shape[1]
+            cols = slice(start, start + src.shape[1])
             nc.vector.quantize_mx(
-                out=words[:, start : start + width].bitcast(FP8X4),
-                scales=scales[:, start : start + width],
-                in_=src[:].rearrange("p c t -> p (c t)"),
+                out=words[:, cols].bitcast(FP8X4), scales=scales[:, cols], in_=src[:].rearrange("p c t -> p (c t)")
             )
 
         def write_z(t, h, src):
             nc.scalar.activation(z_bf[h][:, :, t], src, ACT.Copy, scale=gain[:, t : t + 1])
 
-        low = [sb("low%d" % t, [P, S], F32) for t in range(PACK - 1)]
-        high = [sb("high%d" % t, [P, S], F32) for t in range(PACK - 1)]
+        low = [sb("low%d" % t, [P, S], F32) for t in range(LAST)]
+        high = [sb("high%d" % t, [P, S], F32) for t in range(LAST)]
 
         def fetch_less_a(t, lst, dst):
-            nc.vector.tensor_tensor(dst[t][:], win_d[t][:].indirect(lst[:]), a[t][:], ALU.subtract)
+            nc.vector.tensor_tensor(dst[t][:], second_win[t][:].indirect(lst[:]), a[t][:], ALU.subtract)
 
         def clamp(t):
             nc.vector.scalar_tensor_tensor(low[t][:], low[t][:], 0.0, high[t][:], ALU.min, ALU.max)
-            first, second = (4, 6) if t == 0 else (0, 2)
+
+        def sum_on_tensor(t, first_bank):
             turned = []
             for h in range(2):
-                bank = psum.tile([P, 2, P], F32, name="sum", tag="bank%d" % (first + h))
+                bank = psum_bank(first_bank + h, [P, 2, P])
                 for b in range(2):
                     cols = slice(h * HALF + b * P, h * HALF + (b + 1) * P)
                     nc.tensor.matmul(bank[:, b, :], a[t][:, cols], ident[:], start=True, stop=False, is_transpose=True)
@@ -180,135 +186,134 @@ def tile_picked_twcclampbhopg_none_po_kernel(
                 nc.scalar.copy(tile[:], bank[:])
                 turned.append(tile)
             for h in range(2):
-                bank = psum.tile([P, HALF], F32, name="back", tag="bank%d" % (second + h))
+                bank = psum_bank(first_bank + 2 + h, [P, HALF])
                 for b in range(2):
                     nc.tensor.transpose(bank[:, b * P : (b + 1) * P], turned[h][:, b, :], ident[:])
                 write_z(t, h, bank[:])
 
-        last = PACK - 1
-        low_l = sb("low_l", [P, S], F32)
-        high_l = [sb("high_l0", [P, HALF], F32), sb("high_l1", [P, HALF], F32, "late")]
+        def sum_on_gpsimd(t):
+            for h in range(2):
+                part = low[t][:, half_cols(h)]
+                nc.gpsimd.tensor_tensor(part, part, a[t][:, half_cols(h)], ALU.add)
+                write_z(t, h, part)
 
-        def fetch_high_last(h):
-            nc.vector.tensor_copy(high_l[h][:], win_d[last][:].indirect(entries(l_n3, h * HALF, HALF)))
+        last_high = [sb("last_high%d" % h, [P, HALF], F32) for h in range(2)]
 
-        def max_last(h):
-            part = low_l[:, h * HALF : (h + 1) * HALF]
-            nc.vector.tensor_tensor(part, part, high_l[h][:], ALU.max)
-            write_z(last, h, part)
+        def fetch_last_high(h):
+            nc.vector.tensor_copy(last_high[h][:], second_win[LAST][:].indirect(entries(l_n3, h * HALF, HALF)))
 
         fetch_less_a(0, l_n2, low)
         fetch_less_a(0, l_n3, high)
         fetch_less_a(1, l_n2, low)
         clamp(0)
+        sum_on_tensor(0, PACK)
         fetch_less_a(1, l_n3, high)
-        nc.vector.tensor_copy(low[2][:], win_d[2][:].indirect(l_n2[:]))
+        fetch_less_a(2, l_n2, low)
         clamp(1)
-        nc.vector.tensor_copy(high[2][:], win_d[2][:].indirect(l_n3[:]))
-        nc.vector.tensor_tensor(low[2][:], low[2][:], a[2][:], ALU.min)
-        fetch_a(last, "high1")
-        nc.vector.tensor_tensor(low[2][:], low[2][:], high[2][:], ALU.max)
-        for h in range(2):
-            write_z(2, h, low[2][:, h * HALF : (h + 1) * HALF])
-        nc.vector.tensor_copy(low_l[:], win_d[last][:].indirect(l_n2[:]))
-        fetch_high_last(0)
-        nc.vector.tensor_tensor(low_l[:], low_l[:], a[last][:], ALU.min)
-        fetch_high_last(1)
-        max_last(0)
+        sum_on_tensor(1, 0)
+        fetch_less_a(2, l_n3, high)
+        fetch_a(LAST, "high1")
+        clamp(2)
+        sum_on_gpsimd(2)
+        fetch_last_high(0)
+        last_low = sb("last_low", [P, S], F32, "high2")
+        nc.vector.tensor_copy(last_low[:], second_win[LAST][:].indirect(l_n2[:]))
+        fetch_last_high(1)
+        nc.vector.tensor_tensor(last_low[:], last_low[:], a[LAST][:], ALU.min)
         cand_sc = sb("cand_sc", [P, S], U8)
-        deal(cand_sc[:], cand_sc_raw[:], 16)
-        max_last(1)
+        nc.vector.tensor_copy(
+            cand_sc[:].rearrange("p (t c i) -> p c t i", t=PACK, i=LINE),
+            cand_sc_raw[:].rearrange("p (c i t) -> p c t i", t=PACK, i=LINE),
+        )
+        for h in range(2):
+            part = last_low[:, half_cols(h)]
+            nc.vector.tensor_tensor(part, part, last_high[h][:], ALU.max)
+            write_z(LAST, h, part)
 
-        cand_w = sb("cand_w", [P, S], U32, "late")
+        cand_w = sb("cand_w", [P, S], U32, "last_high1")
         nc.vector.tensor_copy(
             cand_w[:].rearrange("p (t m) -> p m t", t=PACK), x_w[:].bitcast(U32).indirect(l_cand[:])
         )
-        quantize(z_w, z_sc, 0, z_bf[0])
-        quantize(z_w, z_sc, HALF, z_bf[1])
-
-        first_halves = []
         for h in range(2):
-            bank = psum.tile([P, HALF], F32, name="first_half", tag="bank%d" % (PACK * h))
-            cols = slice(h * HALF, (h + 1) * HALF)
-            nc.tensor.matmul_mx(
-                out=bank[:], lhsT=cand_w[:, :P].bitcast(FP8X4), lhsT_scale=cand_sc[:, :P],
-                rhs=z_w[:, cols].bitcast(FP8X4), rhs_scale=z_sc[:, cols], start=True, stop=True,
-            )
-            first_halves.append(bank)
-        banks = {t: product("bank%d" % t, t, cand_w, cand_sc, 0, z_w, z_sc) for t in range(1, PACK)}
+            quantize(z_w, z_sc, h * HALF, z_bf[h])
+
+        first_halves = [
+            product(PACK * h, 0, cand_w, cand_sc, z_w[:, half_cols(h)], z_sc[:, half_cols(h)]) for h in range(2)
+        ]
+        scores = {t: product(t, t, cand_w, cand_sc, z_w[:], z_sc[:]) for t in range(1, PACK)}
         neg_copy = [sb("neg_copy%d" % t, [P, S], F32) for t in range(PACK)]
-        other = [sb("other%d" % t, [P, S], F32) for t in range(PACK)]
+        neg_s0 = sb("neg_s0", [P, S], F32)
+        gates = {t: sb("gate%d" % t, [P, S], F32) for t in range(1, PACK)}
         res = sb("res", [P, PACK, S], F32)
         out_rows = out_0.rearrange("(p t) j -> p t j", t=PACK)
 
         def gate(t):
-            nc.scalar.activation(win_a[t][:, :S], banks[t][:], ACT.Copy, scale=0.0625)
-            nc.scalar.activation(other[t][:], win_a[t][:].indirect(l_n4[:]), ACT.Sigmoid)
+            nc.scalar.activation(first_win[t][:, :S], scores[t][:], ACT.Copy, scale=SCORE_SCALE)
+            nc.scalar.activation(gates[t][:], first_win[t][:].indirect(l_n4[:]), ACT.Sigmoid)
 
-        def gated(t):
-            nc.vector.scalar_tensor_tensor(win_d[t][:, :S], banks[t][:], -0.0625, other[t][:], ALU.mult, ALU.mult)
+        def apply_gate(t):
+            nc.vector.scalar_tensor_tensor(
+                second_win[t][:, :S], scores[t][:], -SCORE_SCALE, gates[t][:], ALU.mult, ALU.mult
+            )
 
-        def duplicate(t, copy):
-            copy(neg_copy[t][:], win_d[t][:, :S])
+        def duplicate(t, copy, cols):
+            copy(neg_copy[t][:, cols], second_win[t][:, cols])
 
         def differ(t, start, count):
             cols = slice(start, start + count)
             nc.vector.tensor_tensor(
-                res[:, t, cols], win_d[t][:].indirect(entries(l_n5, start, count)), neg_copy[t][:, cols], ALU.subtract
+                res[:, t, cols], second_win[t][:].indirect(entries(l_n5, start, count)), neg_copy[t][:, cols],
+                ALU.subtract,
             )
 
-        def store(t0, t1, start, count):
-            cols = slice(start, start + count)
+        def store(t0, t1, cols):
             nc.sync.dma_start(out_rows[:, t0:t1, cols], res[:, t0:t1, cols])
 
         for h in range(2):
-            cols = slice(h * HALF, (h + 1) * HALF)
-            nc.scalar.activation(win_a[0][:, cols], first_halves[h][:], ACT.Sigmoid, scale=0.0625)
-            nc.vector.tensor_scalar(other[0][:, cols], first_halves[h][:], -0.0625, None, ALU.mult)
-        nc.vector.tensor_tensor(win_d[0][:, :S], win_a[0][:].indirect(l_n4[:]), other[0][:], ALU.mult)
-        gate(1)
-        duplicate(0, nc.gpsimd.tensor_copy)
-        gated(1)
-        differ(0, 0, S)
-        store(0, 1, 0, S)
-        gate(2)
-        duplicate(1, nc.gpsimd.tensor_copy)
-        gated(2)
-        differ(1, 0, S)
-        store(1, 2, 0, S)
-        gate(3)
-        gated(3)
-        duplicate(2, nc.scalar.copy)
-        duplicate(3, nc.scalar.copy)
-        differ(2, 0, HALF)
-        differ(3, 0, HALF)
-        store(2, 4, 0, HALF)
+            nc.scalar.activation(first_win[0][:, half_cols(h)], first_halves[h][:], ACT.Sigmoid, scale=SCORE_SCALE)
+            nc.vector.tensor_scalar(neg_s0[:, half_cols(h)], first_halves[h][:], -SCORE_SCALE, None, ALU.mult)
+        nc.vector.tensor_tensor(second_win[0][:, :S], first_win[0][:].indirect(l_n4[:]), neg_s0[:], ALU.mult)
+        every = slice(0, S)
+        for t in range(2):
+            gate(t + 1)
+            duplicate(t, nc.gpsimd.tensor_copy, every)
+            apply_gate(t + 1)
+            differ(t, 0, S)
+            store(t, t + 1, every)
+        gate(LAST)
+        apply_gate(LAST)
+        duplicate(2, nc.scalar.copy, every)
+        for h in range(2):
+            duplicate(LAST, nc.scalar.copy, half_cols(h))
 
         o_w = sb("o_w", [P, S], U32)
         o_sc = sb("o_sc", [P, S], U8)
+        words_out = out_1[0].rearrange("p n t -> p (n t)").bitcast(I32)
+
+        def finish_half(h):
+            for t in range(2, PACK):
+                differ(t, h * HALF, HALF)
+            store(2, PACK, half_cols(h))
 
         def interleave(copy, name, start, count):
             tile = sb(name, [P, count, PACK], BF16)
             copy(
-                tile[:].rearrange("p (c i) t -> p c t i", i=4),
-                res[:, :, start : start + count].rearrange("p t (c i) -> p c t i", i=4),
+                tile[:].rearrange("p (c i) t -> p c t i", i=LINE // 4),
+                res[:, :, start : start + count].rearrange("p t (c i) -> p c t i", i=LINE // 4),
             )
             return tile
 
-        words_out = out_1[0].rearrange("p n t -> p (n t)").bitcast(I32)
+        finish_half(0)
         o_first = interleave(nc.scalar.copy, "o_first", 0, HALF)
-        differ(2, HALF, HALF)
-        differ(3, HALF, HALF)
-        store(2, 4, HALF, HALF)
+        finish_half(1)
         o_last = interleave(nc.scalar.copy, "o_last", HALF + QUARTER, QUARTER)
         o_mid = interleave(nc.vector.tensor_copy, "o_mid", HALF, QUARTER)
-        quantize(o_w, o_sc, 0, o_first)
-        nc.sync.dma_start(words_out[:, :HALF], o_w[:, :HALF].bitcast(I32))
-        quantize(o_w, o_sc, HALF, o_mid)
-        quantize(o_w, o_sc, HALF + QUARTER, o_last)
-        nc.sync.dma_start(words_out[:, HALF:], o_w[:, HALF:].bitcast(I32))
-        for q in range(4):
+        for start, src in ((0, o_first), (HALF, o_mid), (HALF + QUARTER, o_last)):
+            quantize(o_w, o_sc, start, src)
+            cols = slice(start, start + src.shape[1])
+            nc.sync.dma_start(words_out[:, cols], o_w[:, cols].bitcast(I32))
+        for q in range(QUADRANTS):
             queue = nc.scalar if q % 2 else nc.sync
             queue.dma_start(
-                out_2[0, 4 * q : 4 * q + 4, :].bitcast(I32), o_sc[32 * q : 32 * q + 4, :].bitcast(I32)
+                out_2[0, PACK * q : PACK * (q + 1), :].bitcast(I32), o_sc[32 * q : 32 * q + PACK, :].bitcast(I32)
             )

from contextlib import ExitStack

import concourse.mybir as mybir
from concourse.masks import make_identity

K, T, S = 512, 2048, 512
FLOPS = 3 * 2 * K * S * S

F32 = mybir.dt.float32
BF16 = mybir.dt.bfloat16
I32 = mybir.dt.int32
U32 = mybir.dt.uint32
U16 = mybir.dt.uint16
U8 = mybir.dt.uint8
FP8X4 = mybir.dt.float8_e4m3fn_x4
ALU = mybir.AluOpType
ACT = mybir.ActivationFunctionType

P = 128
PACK = 4
QUADRANTS = 4
GROUP = 16
LINE = 16
HALF = S // 2
QUARTER = S // 4
SCORE_SCALE = 0.0625
LAST = PACK - 1


def tile_picked_twcclampbhopg_none_po_kernel(
    tc, x_words, x_scales, w1_words, w1_scales, w2_words, w2_scales, gs,
    offs, two, n1, n2, n3, cand, n4, n5, out_0, out_1, out_2,
):
    nc = tc.nc
    with ExitStack() as ctx:
        keep = ctx.enter_context(tc.tile_pool(name="keep", bufs=1))
        psum = ctx.enter_context(tc.psum_pool(name="psum", bufs=1))

        def sb(name, shape, dtype, tag=None):
            return keep.tile(shape, dtype, name=name, tag=tag or name, align_bytes=64)

        def psum_bank(number, shape):
            return psum.tile(shape, F32, name="bank%d" % number, tag="bank%d" % number)

        def half_cols(h):
            return slice(h * HALF, (h + 1) * HALF)

        def entries(lst, start, count):
            return lst[:, start // GROUP : (start + count) // GROUP]

        def load_list(name, src):
            tile = sb(name, [P, S // GROUP], U16)
            nc.sync.dma_start(tile[:], src)
            return tile

        def load_words(name, src, width):
            tile = sb(name, [P, width], I32)
            nc.sync.dma_start(tile[:], src[0].rearrange("p n t -> p (n t)").bitcast(I32))
            return tile

        def load_scales(name, src, width, queues):
            tile = sb(name, [P, width], U8)
            repeats = P // QUADRANTS // PACK
            for q in range(QUADRANTS):
                rows = src[0, PACK * q : PACK * (q + 1), :].bitcast(I32)
                queues[q % len(queues)].dma_start(
                    tile[32 * q : 32 * (q + 1), :].bitcast(I32),
                    rows.unsqueeze(0).to_broadcast([repeats, PACK, width // 4]),
                )
            return tile

        l_offs = load_list("l_offs", offs)
        x_sc = load_scales("x_sc", x_scales, T, [nc.scalar, nc.sync])
        l_two = load_list("l_two", two)
        x_w = load_words("x_w", x_words, T)
        w1_raw = load_words("w1_raw", w1_words, S)
        w1_sc_raw = load_scales("w1_sc_raw", w1_scales, S, [nc.sync])
        l_cand = load_list("l_cand", cand)
        w2_raw = load_words("w2_raw", w2_words, S)
        w2_sc_raw = load_scales("w2_sc_raw", w2_scales, S, [nc.sync])
        zero = sb("zero", [P, 1], F32)
        nc.vector.memset(zero[:], 0.0)
        ident = sb("ident", [P, P], F32)
        make_identity(nc, ident[:])
        l_n1 = load_list("l_n1", n1)
        l_n2 = load_list("l_n2", n2)
        l_n3 = load_list("l_n3", n3)
        gain = sb("gain", [P, PACK], F32)
        nc.sync.dma_start(gain[:], gs.rearrange("(p t) o -> p (t o)", t=PACK))
        l_n4 = load_list("l_n4", n4)
        l_n5 = load_list("l_n5", n5)

        first_win = [sb("first_win%d" % t, [P, 2 * S], F32) for t in range(PACK)]
        second_win = [sb("second_win%d" % t, [P, 2 * S], F32) for t in range(PACK)]
        for t in range(PACK):
            nc.scalar.activation(first_win[t][:, S:], zero[:].to_broadcast([P, S]), ACT.Sigmoid)

        def pick_scales(name, lst):
            tile = sb(name, [P, S], U8)
            nc.vector.tensor_copy(tile[:], x_sc[:].indirect(lst[:]))
            return tile

        def pick_words(name, lst):
            tile = sb(name, [P, S], U32)
            nc.vector.tensor_copy(tile[:], x_w[:].bitcast(U32).indirect(lst[:]))
            return tile

        def deal_weights(dst, src, t0, t1):
            nc.gpsimd.tensor_copy(
                dst[:].rearrange("p (t m) -> p t m", t=PACK)[:, t0:t1, :],
                src[:].rearrange("p (m t) -> p t m", t=PACK)[:, t0:t1, :],
            )

        def product(bank_number, t, lhs_w, lhs_sc, rhs_w, rhs_sc):
            bank = psum_bank(bank_number, [P, rhs_w.shape[1]])
            cols = slice(t * P, (t + 1) * P)
            nc.tensor.matmul_mx(
                out=bank[:], lhsT=lhs_w[:, cols].bitcast(FP8X4), lhsT_scale=lhs_sc[:, cols],
                rhs=rhs_w.bitcast(FP8X4), rhs_scale=rhs_sc, start=True, stop=True,
            )
            return bank

        idx_sc = pick_scales("idx_sc", l_offs)
        two_sc = pick_scales("two_sc", l_two)
        idx_w = pick_words("idx_w", l_offs)
        w1_w = sb("w1_w", [P, S], I32)
        w1_sc = sb("w1_sc", [P, S], U8)
        for t0, t1 in ((0, 1), (1, PACK)):
            deal_weights(w1_w, w1_raw, t0, t1)
            deal_weights(w1_sc, w1_sc_raw, t0, t1)
        for t in range(PACK):
            bank = product(t, t, w1_w, w1_sc, idx_w[:], idx_sc[:])
            nc.scalar.activation(first_win[t][:, :S], bank[:], ACT.Copy, scale=-0.5)
            nc.scalar.copy(second_win[t][:, S:], bank[:])

        two_w = pick_words("two_w", l_two)
        w2_w = sb("w2_w", [P, S], I32)
        deal_weights(w2_w, w2_raw, 0, PACK)
        w2_sc = sb("w2_sc", [P, S], U8)
        deal_weights(w2_sc, w2_sc_raw, 0, PACK)
        cand_sc_raw = pick_scales("cand_sc_raw", l_cand)
        for t in range(PACK):
            bank = product(PACK + t, t, w2_w, w2_sc, two_w[:], two_sc[:])
            nc.scalar.copy(second_win[t][:, :S], bank[:])

        a = {}

        def fetch_a(t, tag=None):
            a[t] = sb("a%d" % t, [P, S], F32, tag)
            nc.vector.tensor_tensor(a[t][:], first_win[t][:].indirect(l_n1[:]), second_win[t][:, S:], ALU.add)

        for t in range(LAST):
            fetch_a(t)

        z_bf = [sb("z_bf%d" % h, [P, HALF, PACK], BF16) for h in range(2)]
        z_w = sb("z_w", [P, S], U32)
        z_sc = sb("z_sc", [P, S], U8)

        def quantize(words, scales, start, src):
            cols = slice(start, start + src.shape[1])
            nc.vector.quantize_mx(
                out=words[:, cols].bitcast(FP8X4), scales=scales[:, cols], in_=src[:].rearrange("p c t -> p (c t)")
            )

        def write_z(t, h, src):
            nc.scalar.activation(z_bf[h][:, :, t], src, ACT.Copy, scale=gain[:, t : t + 1])

        low = [sb("low%d" % t, [P, S], F32) for t in range(LAST)]
        high = [sb("high%d" % t, [P, S], F32) for t in range(LAST)]

        def fetch_less_a(t, lst, dst):
            nc.vector.tensor_tensor(dst[t][:], second_win[t][:].indirect(lst[:]), a[t][:], ALU.subtract)

        def clamp(t):
            nc.vector.scalar_tensor_tensor(low[t][:], low[t][:], 0.0, high[t][:], ALU.min, ALU.max)

        def sum_on_tensor(t, first_bank):
            turned = []
            for h in range(2):
                bank = psum_bank(first_bank + h, [P, 2, P])
                for b in range(2):
                    cols = slice(h * HALF + b * P, h * HALF + (b + 1) * P)
                    nc.tensor.matmul(bank[:, b, :], a[t][:, cols], ident[:], start=True, stop=False, is_transpose=True)
                    nc.tensor.matmul(bank[:, b, :], low[t][:, cols], ident[:], start=False, stop=True, is_transpose=True)
                tile = sb("turned%d_%d" % (t, h), [P, 2, P], F32)
                nc.scalar.copy(tile[:], bank[:])
                turned.append(tile)
            for h in range(2):
                bank = psum_bank(first_bank + 2 + h, [P, HALF])
                for b in range(2):
                    nc.tensor.transpose(bank[:, b * P : (b + 1) * P], turned[h][:, b, :], ident[:])
                write_z(t, h, bank[:])

        def sum_on_gpsimd(t):
            for h in range(2):
                part = low[t][:, half_cols(h)]
                nc.gpsimd.tensor_tensor(part, part, a[t][:, half_cols(h)], ALU.add)
                write_z(t, h, part)

        last_high = [sb("last_high%d" % h, [P, HALF], F32) for h in range(2)]

        def fetch_last_high(h):
            nc.vector.tensor_copy(last_high[h][:], second_win[LAST][:].indirect(entries(l_n3, h * HALF, HALF)))

        fetch_less_a(0, l_n2, low)
        fetch_less_a(0, l_n3, high)
        fetch_less_a(1, l_n2, low)
        clamp(0)
        sum_on_tensor(0, PACK)
        fetch_less_a(1, l_n3, high)
        fetch_less_a(2, l_n2, low)
        clamp(1)
        sum_on_tensor(1, 0)
        fetch_less_a(2, l_n3, high)
        fetch_a(LAST, "high1")
        clamp(2)
        sum_on_gpsimd(2)
        fetch_last_high(0)
        last_low = sb("last_low", [P, S], F32, "high2")
        nc.vector.tensor_copy(last_low[:], second_win[LAST][:].indirect(l_n2[:]))
        fetch_last_high(1)
        nc.vector.tensor_tensor(last_low[:], last_low[:], a[LAST][:], ALU.min)
        cand_sc = sb("cand_sc", [P, S], U8)
        nc.vector.tensor_copy(
            cand_sc[:].rearrange("p (t c i) -> p c t i", t=PACK, i=LINE),
            cand_sc_raw[:].rearrange("p (c i t) -> p c t i", t=PACK, i=LINE),
        )
        for h in range(2):
            part = last_low[:, half_cols(h)]
            nc.vector.tensor_tensor(part, part, last_high[h][:], ALU.max)
            write_z(LAST, h, part)

        cand_w = sb("cand_w", [P, S], U32, "last_high1")
        nc.vector.tensor_copy(
            cand_w[:].rearrange("p (t m) -> p m t", t=PACK), x_w[:].bitcast(U32).indirect(l_cand[:])
        )
        for h in range(2):
            quantize(z_w, z_sc, h * HALF, z_bf[h])

        first_halves = [
            product(PACK * h, 0, cand_w, cand_sc, z_w[:, half_cols(h)], z_sc[:, half_cols(h)]) for h in range(2)
        ]
        scores = {t: product(t, t, cand_w, cand_sc, z_w[:], z_sc[:]) for t in range(1, PACK)}
        neg_copy = [sb("neg_copy%d" % t, [P, S], F32) for t in range(PACK)]
        neg_s0 = sb("neg_s0", [P, S], F32)
        gates = {t: sb("gate%d" % t, [P, S], F32) for t in range(1, PACK)}
        res = sb("res", [P, PACK, S], F32)
        out_rows = out_0.rearrange("(p t) j -> p t j", t=PACK)

        def gate(t):
            nc.scalar.activation(first_win[t][:, :S], scores[t][:], ACT.Copy, scale=SCORE_SCALE)
            nc.scalar.activation(gates[t][:], first_win[t][:].indirect(l_n4[:]), ACT.Sigmoid)

        def apply_gate(t):
            nc.vector.scalar_tensor_tensor(
                second_win[t][:, :S], scores[t][:], -SCORE_SCALE, gates[t][:], ALU.mult, ALU.mult
            )

        def duplicate(t, copy, cols):
            copy(neg_copy[t][:, cols], second_win[t][:, cols])

        def differ(t, start, count):
            cols = slice(start, start + count)
            nc.vector.tensor_tensor(
                res[:, t, cols], second_win[t][:].indirect(entries(l_n5, start, count)), neg_copy[t][:, cols],
                ALU.subtract,
            )

        def store(t0, t1, cols):
            nc.sync.dma_start(out_rows[:, t0:t1, cols], res[:, t0:t1, cols])

        for h in range(2):
            nc.scalar.activation(first_win[0][:, half_cols(h)], first_halves[h][:], ACT.Sigmoid, scale=SCORE_SCALE)
            nc.vector.tensor_scalar(neg_s0[:, half_cols(h)], first_halves[h][:], -SCORE_SCALE, None, ALU.mult)
        nc.vector.tensor_tensor(second_win[0][:, :S], first_win[0][:].indirect(l_n4[:]), neg_s0[:], ALU.mult)
        every = slice(0, S)
        for t in range(2):
            gate(t + 1)
            duplicate(t, nc.gpsimd.tensor_copy, every)
            apply_gate(t + 1)
            differ(t, 0, S)
            store(t, t + 1, every)
        gate(LAST)
        apply_gate(LAST)
        duplicate(2, nc.scalar.copy, every)
        for h in range(2):
            duplicate(LAST, nc.scalar.copy, half_cols(h))

        o_w = sb("o_w", [P, S], U32)
        o_sc = sb("o_sc", [P, S], U8)
        words_out = out_1[0].rearrange("p n t -> p (n t)").bitcast(I32)

        def finish_half(h):
            for t in range(2, PACK):
                differ(t, h * HALF, HALF)
            store(2, PACK, half_cols(h))

        def interleave(copy, name, start, count):
            tile = sb(name, [P, count, PACK], BF16)
            copy(
                tile[:].rearrange("p (c i) t -> p c t i", i=LINE // 4),
                res[:, :, start : start + count].rearrange("p t (c i) -> p c t i", i=LINE // 4),
            )
            return tile

        finish_half(0)
        o_first = interleave(nc.scalar.copy, "o_first", 0, HALF)
        finish_half(1)
        o_last = interleave(nc.scalar.copy, "o_last", HALF + QUARTER, QUARTER)
        o_mid = interleave(nc.vector.tensor_copy, "o_mid", HALF, QUARTER)
        for start, src in ((0, o_first), (HALF, o_mid), (HALF + QUARTER, o_last)):
            quantize(o_w, o_sc, start, src)
            cols = slice(start, start + src.shape[1])
            nc.sync.dma_start(words_out[:, cols], o_w[:, cols].bitcast(I32))
        for q in range(QUADRANTS):
            queue = nc.scalar if q % 2 else nc.sync
            queue.dma_start(
                out_2[0, PACK * q : PACK * (q + 1), :].bitcast(I32), o_sc[32 * q : 32 * q + PACK, :].bitcast(I32)
            )
